import numpy as np
CORES = [4,20,36,52,68,84,100,116,132,148,164,180,196,212,228,244]
N = 16
TK = 64
def setup_inputs(rng):
    return {"b": rng.standard_normal((N, 128, TK), dtype=np.float32), "l": (rng.standard_normal((N, 128, N * 128), dtype=np.float32) / 16)}
def setup_inputs_big(rng):
    d = setup_inputs(rng)
    for k in ("b",): d[k] = (d[k].astype(np.float32) * 1048576.0).astype(d[k].dtype)
    return d
def setup_inputs_small(rng):
    d = setup_inputs(rng)
    for k in ("b",): d[k] = (d[k].astype(np.float32) * (1 / 1048576.0)).astype(d[k].dtype)
    return d
def setup_inputs_apart(rng):
    d = setup_inputs(rng)
    f = (10.0 ** rng.permutation(np.linspace(-1.5, 1.5, N))).astype(np.float32).reshape(N, 1, 1)
    for k in ("b",): d[k] = (d[k].astype(np.float32) * f).astype(d[k].dtype)
    return d
def reference(b, l):
    B, L = b.astype(np.float64), l.astype(np.float64)
    y = np.zeros((N, 128, TK))
    for r in range(N):
        acc = B[r].copy()
        for s in range(r):
            acc -= L[r][:, 128 * s:128 * s + 128].T @ y[s]
        y[r] = acc
    return {"y": y.astype(np.float32)}

@@ -1,0 +1,240 @@
+import numpy as np
+from concourse.bass import DstId, RemoteDMATransfer
+from concourse.mybir import AluOpType
+
+N, TK, P = 16, 64, 128
+GROUPS = [4, 4, 4, 4]
+WINDOW = [0, 1, 1, 1]
+NW = 6
+
+
+def _plan():
+    gs, s = [], 0
+    for G in GROUPS:
+        gs.append(s)
+        s += G
+    info = []
+    for J, G in enumerate(GROUPS):
+        for i in range(G):
+            info.append((J, gs[J], G, i, gs[max(0, J - WINDOW[J])]))
+    return gs, info
+
+
+GS, INFO = _plan()
+
+
+def _split(a, b):
+    return [(c0, min(c0 + 4, b)) for c0 in range(a, b, 4)]
+
+
+def _chunks(m):
+    J, g, G, i, w = INFO[m]
+    if i == G - 1:
+        return []
+    return _split(g, m) + _split(w, g)
+
+
+def _chunk_of(m, c):
+    for k, (c0, c1) in enumerate(_chunks(m)):
+        if c0 <= c < c1:
+            return k
+    return None
+
+
+GMAX = max(GROUPS)
+MAXW = max([1] + [m - INFO[m][4] for m in range(N) if _chunks(m)])
+MAXK = max([1] + [len(_chunks(m)) for m in range(N)])
+
+SCRATCH = {
+    "L": ("sbuf", [P, P * (N - 1)], "float32"),
+    "X": ("sbuf", [P, P * (N - 1)], "float32"),
+    "AT": ("sbuf", [P, P * MAXW], "float32"),
+    "AR": ("sbuf", [P, P * MAXW * max(1, GMAX - 1)], "float32"),
+    "Y": ("sbuf", [P, TK * N], "float32"),
+    "PR": ("sbuf", [P, TK * max(1, GMAX - 1)], "float32"),
+    "bb": ("sbuf", [P, TK], "float32"),
+    "pp": ("sbuf", [P, TK], "float32"),
+    "seed": ("sbuf", [P, P + 1], "float32"),
+    "dz": ("dram", [1, P * (P + 1)], "float32"),
+    "eye": ("sbuf", [P, P], "float32"),
+    "acc": ("psum", [P, 512], "float32"),
+    "accf": ("psum", [P, 512], "float32"),
+}
+for _k in range(NW):
+    SCRATCH["wk%d" % _k] = ("psum", [P, 512], "float32")
+
+SEMAPHORES = (["lb", "ey", "ez", "ms", "ls", "st", "pa", "pf", "vp", "vy"]
+              + ["l%d" % k for k in range(4)] + ["y%d" % s for s in range(N)]
+              + ["p%d" % i for i in range(max(1, GMAX - 1))]
+              + ["a%d_%d" % (i, k) for i in range(max(1, GMAX - 1)) for k in range(MAXK)]
+              + ["pw%d" % k for k in range(NW)] + ["vw%d" % k for k in range(NW)])
+
+
+def rank_program(g, core, T, topo):
+    t = T.rank_of(core)
+    if t is None:
+        return
+    cores = T.cores
+    J, g0, G, i, w = INFO[t]
+    te, ve, sy, sc = g.tensor, g.vector, g.sync, g.scalar
+    qn = {"g": g, "t": te, "v": ve, "s": sy, "c": sc}
+    seen = {}
+
+    def wait(q, name, val):
+        if seen.get((q, name), 0) < val:
+            seen[(q, name)] = val
+            qn[q].wait_ge(T.sem[name], val)
+
+    def mask_of(src, dests):
+        m = topo.mask(cores[src], cores[dests[0]])
+        for d in dests[1:]:
+            m &= topo.mask(cores[src], cores[d])
+        return m
+
+    def count(src, dests):
+        return bin(mask_of(src, dests)).count("1")
+
+    def later(m):
+        return list(range(m + 1, INFO[m][1] + INFO[m][2]))
+
+    def group(K):
+        return list(range(GS[K], GS[K] + GROUPS[K]))
+
+    sent = [0]
+
+    def send(src_ap, dst_ap, dests, sem):
+        ids = []
+        for d in dests:
+            rid, pid = topo.addr(cores[d], core)
+            ids.append(DstId(rid=rid, pnc=pid))
+        m = mask_of(t, dests)
+        g.remote_dma_fused([RemoteDMATransfer(dst_ids=ids, dma_engine_mask=m, remote_sem=T.sem[sem], srcs=[src_ap],
+                                              dsts=[dst_ap for _ in dests], alu_op=0)], local_sem=T.sem.ls)
+        sent[0] += bin(m).count("1")
+
+    def tile(buf, c):
+        return buf[:, P * c:P * (c + 1)]
+
+    def vec(buf, k):
+        return buf[:, TK * k:TK * (k + 1)]
+
+    mine = _chunks(t)
+    sy.dma_start(T.bb[:, :], T.b[:, :]).then_inc(T.sem.lb, 16)
+    if mine:
+        ve.memset(T.seed[:, 1:P + 1], 0.0).then_inc(T.sem.ms, 1)
+        ve.memset(T.seed[:, 0:1], 1.0).then_inc(T.sem.ms, 1)
+        wait("s", "ms", 2)
+        sy.dma_start(T.dz[0], T.seed[:, :]).then_inc(T.sem.ez, 16)
+    for n, k in enumerate(list(range((t + 3) // 4))[::-1]):
+        a, b = 512 * k, min(512 * (k + 1), P * t)
+        (sc if n % 2 == 0 else sy).dma_start(T.L[:, a:b], T.l[:, a:b]).then_inc(T.sem["l%d" % k], 16)
+    if mine:
+        wait("s", "ez", 16)
+        sy.dma_start(T.eye[:, :], T.dz[0, 0:P * P]).then_inc(T.sem.ey, 16)
+
+    nb = [0]
+    pwc, vwc = [0] * NW, [0] * NW
+
+    def bank():
+        k = nb[0] % NW
+        nb[0] += 1
+        wait("t", "vw%d" % k, vwc[k])
+        return k
+
+    ready = {}
+
+    def modified(c):
+        return i > 0 and w <= c <= t - 2
+
+    def xt(q, c):
+        if modified(c):
+            wait(q, ready[c][0], ready[c][1])
+            return tile(T.X, c)
+        wait(q, "l%d" % (c // 4), 16)
+        return tile(T.L, c)
+
+    gsend = []
+    far = list(range(0, w))
+    if i < G - 1 and not far:
+        gsend.append(("lb", 16, T.bb[:, :], vec(T.PR, i), later(t), "p%d" % i))
+
+    for k, (c0, c1) in enumerate(mine):
+        bk = bank()
+        ps = T["wk%d" % bk]
+        wait("t", "ey", 16)
+        for j, c in enumerate(range(c0, c1)):
+            wait("t", "l%d" % (c // 4), 16)
+            te.matmul(tile(ps, j), tile(T.L, c), T.eye[:, :], start=True, stop=True).then_inc(T.sem["pw%d" % bk], 1)
+            pwc[bk] += 1
+        wait("v", "pw%d" % bk, pwc[bk])
+        ve.tensor_copy(T.AT[:, P * (c0 - w):P * (c1 - w)], ps[:, 0:P * (c1 - c0)]).then_inc(T.sem["vw%d" % bk], 1)
+        vwc[bk] += 1
+        gsend.append(("vw%d" % bk, vwc[bk], T.AT[:, P * (c0 - w):P * (c1 - w)],
+                      T.AR[:, P * (MAXW * i + c0 - w):P * (MAXW * i + c1 - w)], later(t), "a%d_%d" % (i, k)))
+
+    if i > 0:
+        batches = [(c, c + 1) for c in range(t - 2, g0 - 1, -1)] + _split(w, g0)
+        for c0, c1 in batches:
+            bk = bank()
+            ps = T["wk%d" % bk]
+            for j, c in enumerate(range(c0, c1)):
+                ms = list(range(max(c + 1, g0), t))
+                for m in ms:
+                    wait("t", "a%d_%d" % (m - g0, _chunk_of(m, c)), count(m, later(m)))
+                    rhs = xt("t", m)
+                    te.matmul(tile(ps, j), tile(T.AR, MAXW * (m - g0) + c - w), rhs, start=(m == ms[0]),
+                              stop=(m == ms[-1])).then_inc(T.sem["pw%d" % bk], 1)
+                    pwc[bk] += 1
+                wait("v", "l%d" % (c // 4), 16)
+            wait("v", "pw%d" % bk, pwc[bk])
+            ve.tensor_tensor(T.X[:, P * c0:P * c1], T.L[:, P * c0:P * c1], ps[:, 0:P * (c1 - c0)],
+                             op=AluOpType.subtract).then_inc(T.sem["vw%d" % bk], 1)
+            vwc[bk] += 1
+            for c in range(c0, c1):
+                ready[c] = ("vw%d" % bk, vwc[bk])
+
+    def ysem(c):
+        wait("t", "y%d" % c, count(c, group(J)))
+
+    pbuf, psem = T.bb, ("lb", 16)
+    if far:
+        for c in far:
+            ysem(c)
+            lhs = xt("t", c)
+            te.matmul(T.accf[:, 0:TK], lhs, vec(T.Y, c), start=(c == far[0]), stop=(c == far[-1])).then_inc(T.sem.pf, 1)
+        wait("v", "pf", len(far))
+        wait("v", "lb", 16)
+        ve.tensor_tensor(T.pp[:, :], T.bb[:, :], T.accf[:, 0:TK], op=AluOpType.subtract).then_inc(T.sem.vp, 1)
+        pbuf, psem = T.pp, ("vp", 1)
+        if i < G - 1:
+            gsend.append(("vp", 1, T.pp[:, :], vec(T.PR, i), later(t), "p%d" % i))
+
+    inq = [("p", q) for q in range(g0, t)]
+    win = [("y", c) for c in range(w, g0)]
+    near = (win + inq) if far else (inq + win)
+    ybuf, ysm = pbuf[:, :], psem
+    for n, (kind, c) in enumerate(near):
+        if kind == "p":
+            wait("t", "p%d" % (c - g0), count(c, later(c)))
+            rhs = vec(T.PR, c - g0)
+        else:
+            ysem(c)
+            rhs = vec(T.Y, c)
+        lhs = xt("t", c)
+        te.matmul(T.acc[:, 0:TK], lhs, rhs, start=(n == 0), stop=(n == len(near) - 1)).then_inc(T.sem.pa, 1)
+    if near:
+        wait("v", "pa", len(near))
+        wait("v", psem[0], psem[1])
+        ve.tensor_tensor(vec(T.Y, t), pbuf[:, :], T.acc[:, 0:TK], op=AluOpType.subtract).then_inc(T.sem.vy, 1)
+        ybuf, ysm = vec(T.Y, t), ("vy", 1)
+
+    wait("s", ysm[0], ysm[1])
+    sy.dma_start(T.y[:, :], ybuf).then_inc(T.sem.st, 16)
+    for K in range(J + 1, len(GROUPS)):
+        gsend.append((ysm[0], ysm[1], ybuf, vec(T.Y, t), group(K), "y%d" % t))
+    for sem, val, src, dst, dests, rsem in gsend:
+        wait("g", sem, val)
+        send(src, dst, dests, rsem)
+    if sent[0]:
+        wait("g", "ls", sent[0])
+    wait("s", "st", 16)

@@ -23,8 +23,8 @@ def _plan():
 GS, INFO = _plan()
 
 
-def _split(a, b):
-    return [(c0, min(c0 + 4, b)) for c0 in range(a, b, 4)]
+def _split(a, b, n=4):
+    return [(c0, min(c0 + n, b)) for c0 in range(a, b, n)]
 
 
 def _chunks(m):
@@ -156,7 +156,7 @@ def rank_program(g, core, T, topo):
     gsend = []
     far = list(range(0, w))
     if i < G - 1 and not far:
-        gsend.append(("lb", 16, T.bb[:, :], vec(T.PR, i), later(t), "p%d" % i))
+        gsend.append(("lb", 16, T.bb[:, :], vec(T.PR, i), later(t)[::-1], "p%d" % i))
 
     for k, (c0, c1) in enumerate(mine):
         bk = bank()
@@ -173,24 +173,23 @@ def rank_program(g, core, T, topo):
                       T.AR[:, P * (MAXW * i + c0 - w):P * (MAXW * i + c1 - w)], later(t), "a%d_%d" % (i, k)))
 
     if i > 0:
-        batches = [(c, c + 1) for c in range(t - 2, g0 - 1, -1)] + _split(w, g0)
-        for c0, c1 in batches:
-            bk = bank()
-            ps = T["wk%d" % bk]
-            for j, c in enumerate(range(c0, c1)):
-                ms = list(range(max(c + 1, g0), t))
-                for m in ms:
+        for c0, c1 in [(c, c + 1) for c in range(t - 2, g0 - 1, -1)] + _split(w, g0):
+            cols = list(range(c0, c1))
+            bks = [bank() for c in cols]
+            ms = list(range(t - 1, max(c1, g0) - 1, -1))
+            for m in ms:
+                for bk, c in zip(bks, cols):
                     wait("t", "a%d_%d" % (m - g0, _chunk_of(m, c)), count(m, later(m)))
                     rhs = xt("t", m)
-                    te.matmul(tile(ps, j), tile(T.AR, MAXW * (m - g0) + c - w), rhs, start=(m == ms[0]),
+                    te.matmul(tile(T["wk%d" % bk], 0), tile(T.AR, MAXW * (m - g0) + c - w), rhs, start=(m == ms[0]),
                               stop=(m == ms[-1])).then_inc(T.sem["pw%d" % bk], 1)
                     pwc[bk] += 1
+            for bk, c in zip(bks, cols):
                 wait("v", "l%d" % (c // 4), 16)
-            wait("v", "pw%d" % bk, pwc[bk])
-            ve.tensor_tensor(T.X[:, P * c0:P * c1], T.L[:, P * c0:P * c1], ps[:, 0:P * (c1 - c0)],
-                             op=AluOpType.subtract).then_inc(T.sem["vw%d" % bk], 1)
-            vwc[bk] += 1
-            for c in range(c0, c1):
+                wait("v", "pw%d" % bk, pwc[bk])
+                ve.tensor_tensor(tile(T.X, c), tile(T.L, c), tile(T["wk%d" % bk], 0),
+                                 op=AluOpType.subtract).then_inc(T.sem["vw%d" % bk], 1)
+                vwc[bk] += 1
                 ready[c] = ("vw%d" % bk, vwc[bk])
 
     def ysem(c):
@@ -207,7 +206,7 @@ def rank_program(g, core, T, topo):
         ve.tensor_tensor(T.pp[:, :], T.bb[:, :], T.accf[:, 0:TK], op=AluOpType.subtract).then_inc(T.sem.vp, 1)
         pbuf, psem = T.pp, ("vp", 1)
         if i < G - 1:
-            gsend.append(("vp", 1, T.pp[:, :], vec(T.PR, i), later(t), "p%d" % i))
+            gsend.append(("vp", 1, T.pp[:, :], vec(T.PR, i), later(t)[::-1], "p%d" % i))
 
     inq = [("p", q) for q in range(g0, t)]
     win = [("y", c) for c in range(w, g0)]
@@ -231,7 +230,7 @@ def rank_program(g, core, T, topo):
     wait("s", ysm[0], ysm[1])
     sy.dma_start(T.y[:, :], ybuf).then_inc(T.sem.st, 16)
     for K in range(J + 1, len(GROUPS)):
-        gsend.append((ysm[0], ysm[1], ybuf, vec(T.Y, t), group(K), "y%d" % t))
+        gsend.append((ysm[0], ysm[1], ybuf, vec(T.Y, t), group(K)[::-1] if K == J + 1 else group(K), "y%d" % t))
     for sem, val, src, dst, dests, rsem in gsend:
         wait("g", sem, val)
         send(src, dst, dests, rsem)

@@ -23,6 +23,20 @@ def _plan():
 GS, INFO = _plan()
 
 
+def _relays():
+    r, nG = {}, len(GROUPS)
+    if nG > 2 and GROUPS[0] > 1:
+        r[(0, 2)] = GS[0] + GROUPS[0] - 1
+    for J in range(1, nG - 1):
+        c = J - 1
+        if c < GROUPS[0] and nG - 1 > J and (c, nG - 1) not in r and (c, J) not in r:
+            r[(c, nG - 1)] = GS[J] + GROUPS[J] - 1
+    return r
+
+
+RELAY = _relays()
+
+
 def _split(a, b, n=4):
     return [(c0, min(c0 + n, b)) for c0 in range(a, b, n)]
 
@@ -54,8 +68,8 @@ SCRATCH = {
     "PR": ("sbuf", [P, TK * max(1, GMAX - 1)], "float32"),
     "bb": ("sbuf", [P, TK], "float32"),
     "pp": ("sbuf", [P, TK], "float32"),
-    "seed": ("sbuf", [P, P + 1], "float32"),
-    "dz": ("dram", [1, P * (P + 1)], "float32"),
+    "tri": ("sbuf", [P, 17], "float32"),
+    "strip": ("sbuf", [P, 2 * P], "bfloat16"),
     "eye": ("sbuf", [P, P], "float32"),
     "acc": ("psum", [P, 512], "float32"),
     "accf": ("psum", [P, 512], "float32"),
@@ -63,7 +77,7 @@ SCRATCH = {
 for _k in range(NW):
     SCRATCH["wk%d" % _k] = ("psum", [P, 512], "float32")
 
-SEMAPHORES = (["lb", "ey", "ez", "ms", "ls", "st", "pa", "pf", "vp", "vy"]
+SEMAPHORES = (["lb", "ms", "ls", "st", "pa", "pf", "vp", "vy"]
               + ["l%d" % k for k in range(4)] + ["y%d" % s for s in range(N)]
               + ["p%d" % i for i in range(max(1, GMAX - 1))]
               + ["a%d_%d" % (i, k) for i in range(max(1, GMAX - 1)) for k in range(MAXK)]
@@ -120,18 +134,9 @@ def rank_program(g, core, T, topo):
 
     mine = _chunks(t)
     sy.dma_start(T.bb[:, :], T.b[:, :]).then_inc(T.sem.lb, 16)
-    if mine:
-        ve.memset(T.seed[:, 1:P + 1], 0.0).then_inc(T.sem.ms, 1)
-        ve.memset(T.seed[:, 0:1], 1.0).then_inc(T.sem.ms, 1)
-        wait("s", "ms", 2)
-        sy.dma_start(T.dz[0], T.seed[:, :]).then_inc(T.sem.ez, 16)
     for n, k in enumerate(list(range((t + 3) // 4))[::-1]):
         a, b = 512 * k, min(512 * (k + 1), P * t)
         (sc if n % 2 == 0 else sy).dma_start(T.L[:, a:b], T.l[:, a:b]).then_inc(T.sem["l%d" % k], 16)
-    if mine:
-        wait("s", "ez", 16)
-        sy.dma_start(T.eye[:, :], T.dz[0, 0:P * P]).then_inc(T.sem.ey, 16)
-
     nb = [0]
     pwc, vwc = [0] * NW, [0] * NW
 
@@ -157,11 +162,35 @@ def rank_program(g, core, T, topo):
     far = list(range(0, w))
     if i < G - 1 and not far:
         gsend.append(("lb", 16, T.bb[:, :], vec(T.PR, i), later(t)[::-1], "p%d" % i))
+    for (c, D), R in sorted(RELAY.items()):
+        if R == t and INFO[c][0] == J:
+            gsend.append(("p%d" % (c - g0), count(c, later(c)), vec(T.PR, c - g0), vec(T.Y, c), group(D), "y%d" % c))
+        elif R == t:
+            gsend.append(("y%d" % c, count(c, group(J)), vec(T.Y, c), vec(T.Y, c), group(D), "y%d" % c))
+
+    if mine:
+        B = 16
+        ve.memset(T.strip[0:B, :], 0.0).then_inc(T.sem.ms, 1)
+        ve.memset(T.tri[0:B, :], 0.0).then_inc(T.sem.ms, 1)
+        wait("v", "ms", 2)
+        for c in range(B):
+            ve.memset(T.tri[0:c + 1, c + 1:c + 2], 1.0).then_inc(T.sem.ms, 1)
+        wait("v", "ms", B + 2)
+        ve.tensor_tensor(T.strip[0:B, P:P + B], T.tri[0:B, 1:B + 1], T.tri[0:B, 0:B], op=AluOpType.subtract).then_inc(T.sem.ms, 1)
+        wait("t", "ms", B + 3)
+        bk = bank()
+        for off in range(0, P, B):
+            s = T.strip[0:B, P - off:2 * P - off]
+            te.matmul(tile(T["wk%d" % bk], 0), s, s, start=(off == 0), stop=(off == P - B)).then_inc(T.sem["pw%d" % bk], 1)
+            pwc[bk] += 1
+        wait("v", "pw%d" % bk, pwc[bk])
+        ve.tensor_copy(T.eye[:, :], tile(T["wk%d" % bk], 0)).then_inc(T.sem["vw%d" % bk], 1)
+        vwc[bk] += 1
+        wait("t", "vw%d" % bk, vwc[bk])
 
     for k, (c0, c1) in enumerate(mine):
         bk = bank()
         ps = T["wk%d" % bk]
-        wait("t", "ey", 16)
         for j, c in enumerate(range(c0, c1)):
             wait("t", "l%d" % (c // 4), 16)
             te.matmul(tile(ps, j), tile(T.L, c), T.eye[:, :], start=True, stop=True).then_inc(T.sem["pw%d" % bk], 1)
@@ -193,7 +222,7 @@ def rank_program(g, core, T, topo):
                 ready[c] = ("vw%d" % bk, vwc[bk])
 
     def ysem(c):
-        wait("t", "y%d" % c, count(c, group(J)))
+        wait("t", "y%d" % c, count(RELAY.get((c, J), c), group(J)))
 
     pbuf, psem = T.bb, ("lb", 16)
     if far:
@@ -230,6 +259,8 @@ def rank_program(g, core, T, topo):
     wait("s", ysm[0], ysm[1])
     sy.dma_start(T.y[:, :], ybuf).then_inc(T.sem.st, 16)
     for K in range(J + 1, len(GROUPS)):
+        if (t, K) in RELAY:
+            continue
         gsend.append((ysm[0], ysm[1], ybuf, vec(T.Y, t), group(K)[::-1] if K == J + 1 else group(K), "y%d" % t))
     for sem, val, src, dst, dests, rsem in gsend:
         wait("g", sem, val)

@@ -3,7 +3,7 @@ from concourse.bass import DstId, RemoteDMATransfer
 from concourse.mybir import AluOpType
 
 N, TK, P = 16, 64, 128
-GROUPS = [4, 4, 4, 4]
+GROUPS = [5, 3, 4, 4]
 WINDOW = [0, 1, 1, 1]
 NW = 6
 
@@ -68,8 +68,6 @@ SCRATCH = {
     "PR": ("sbuf", [P, TK * max(1, GMAX - 1)], "float32"),
     "bb": ("sbuf", [P, TK], "float32"),
     "pp": ("sbuf", [P, TK], "float32"),
-    "tri": ("sbuf", [P, 17], "float32"),
-    "strip": ("sbuf", [P, 2 * P], "bfloat16"),
     "eye": ("sbuf", [P, P], "float32"),
     "acc": ("psum", [P, 512], "float32"),
     "accf": ("psum", [P, 512], "float32"),
@@ -77,7 +75,7 @@ SCRATCH = {
 for _k in range(NW):
     SCRATCH["wk%d" % _k] = ("psum", [P, 512], "float32")
 
-SEMAPHORES = (["lb", "ms", "ls", "st", "pa", "pf", "vp", "vy"]
+SEMAPHORES = (["lb", "ms", "idn", "ls", "st", "pa", "pf", "vp", "vy"]
               + ["l%d" % k for k in range(4)] + ["y%d" % s for s in range(N)]
               + ["p%d" % i for i in range(max(1, GMAX - 1))]
               + ["a%d_%d" % (i, k) for i in range(max(1, GMAX - 1)) for k in range(MAXK)]
@@ -168,96 +166,125 @@ def rank_program(g, core, T, topo):
         elif R == t:
             gsend.append(("y%d" % c, count(c, group(J)), vec(T.Y, c), vec(T.Y, c), group(D), "y%d" % c))
 
-    if mine:
-        B = 16
-        ve.memset(T.strip[0:B, :], 0.0).then_inc(T.sem.ms, 1)
-        ve.memset(T.tri[0:B, :], 0.0).then_inc(T.sem.ms, 1)
-        wait("v", "ms", 2)
-        for c in range(B):
-            ve.memset(T.tri[0:c + 1, c + 1:c + 2], 1.0).then_inc(T.sem.ms, 1)
-        wait("v", "ms", B + 2)
-        ve.tensor_tensor(T.strip[0:B, P:P + B], T.tri[0:B, 1:B + 1], T.tri[0:B, 0:B], op=AluOpType.subtract).then_inc(T.sem.ms, 1)
-        wait("t", "ms", B + 3)
-        bk = bank()
-        for off in range(0, P, B):
-            s = T.strip[0:B, P - off:2 * P - off]
-            te.matmul(tile(T["wk%d" % bk], 0), s, s, start=(off == 0), stop=(off == P - B)).then_inc(T.sem["pw%d" % bk], 1)
-            pwc[bk] += 1
-        wait("v", "pw%d" % bk, pwc[bk])
-        ve.tensor_copy(T.eye[:, :], tile(T["wk%d" % bk], 0)).then_inc(T.sem["vw%d" % bk], 1)
-        vwc[bk] += 1
-        wait("t", "vw%d" % bk, vwc[bk])
+    ybuf, ysm = T.bb[:, :], ("lb", 16)
 
-    for k, (c0, c1) in enumerate(mine):
-        bk = bank()
-        ps = T["wk%d" % bk]
-        for j, c in enumerate(range(c0, c1)):
-            wait("t", "l%d" % (c // 4), 16)
-            te.matmul(tile(ps, j), tile(T.L, c), T.eye[:, :], start=True, stop=True).then_inc(T.sem["pw%d" % bk], 1)
+    if J == 0:
+        for k, (c0, c1) in enumerate(mine):
+            gsend.append(("l%d" % (c0 // 4), 16, T.L[:, P * c0:P * c1], T.AR[:, P * (MAXW * i + c0):P * (MAXW * i + c1)],
+                          later(t)[::-1], "a%d_%d" % (i, k)))
+        seq = [(t, 0)] if t >= 1 else []
+        for q in range(1, t + 1):
+            for c in range(q):
+                if (q, c) not in seq:
+                    seq.append((q, c))
+        left = {q: q for q in range(1, t + 1)}
+        rowbank, done = {}, {}
+        for q, c in seq:
+            first = q not in rowbank
+            if first:
+                rowbank[q] = bank()
+            bk = rowbank[q]
+            if q == t:
+                wait("t", "l%d" % (c // 4), 16)
+                lhs = tile(T.L, c)
+            else:
+                wait("t", "a%d_%d" % (q, _chunk_of(q, c)), count(q, later(q)))
+                lhs = tile(T.AR, MAXW * q + c)
+            if c == 0:
+                wait("t", "p0", count(0, later(0)))
+                rhs = vec(T.PR, 0)
+            else:
+                wait("t", done[c][0], done[c][1])
+                rhs = vec(T.Y, c)
+            left[q] -= 1
+            te.matmul(T["wk%d" % bk][:, 0:TK], lhs, rhs, start=first, stop=(left[q] == 0)).then_inc(T.sem["pw%d" % bk], 1)
             pwc[bk] += 1
-        wait("v", "pw%d" % bk, pwc[bk])
-        ve.tensor_copy(T.AT[:, P * (c0 - w):P * (c1 - w)], ps[:, 0:P * (c1 - c0)]).then_inc(T.sem["vw%d" % bk], 1)
-        vwc[bk] += 1
-        gsend.append(("vw%d" % bk, vwc[bk], T.AT[:, P * (c0 - w):P * (c1 - w)],
-                      T.AR[:, P * (MAXW * i + c0 - w):P * (MAXW * i + c1 - w)], later(t), "a%d_%d" % (i, k)))
-
-    if i > 0:
-        for c0, c1 in [(c, c + 1) for c in range(t - 2, g0 - 1, -1)] + _split(w, g0):
-            cols = list(range(c0, c1))
-            bks = [bank() for c in cols]
-            ms = list(range(t - 1, max(c1, g0) - 1, -1))
-            for m in ms:
-                for bk, c in zip(bks, cols):
-                    wait("t", "a%d_%d" % (m - g0, _chunk_of(m, c)), count(m, later(m)))
-                    rhs = xt("t", m)
-                    te.matmul(tile(T["wk%d" % bk], 0), tile(T.AR, MAXW * (m - g0) + c - w), rhs, start=(m == ms[0]),
-                              stop=(m == ms[-1])).then_inc(T.sem["pw%d" % bk], 1)
-                    pwc[bk] += 1
-            for bk, c in zip(bks, cols):
-                wait("v", "l%d" % (c // 4), 16)
+            if left[q] == 0:
                 wait("v", "pw%d" % bk, pwc[bk])
-                ve.tensor_tensor(tile(T.X, c), tile(T.L, c), tile(T["wk%d" % bk], 0),
-                                 op=AluOpType.subtract).then_inc(T.sem["vw%d" % bk], 1)
+                if q == t:
+                    wait("v", "lb", 16)
+                    bq = T.bb[:, :]
+                else:
+                    wait("v", "p%d" % q, count(q, later(q)))
+                    bq = vec(T.PR, q)
+                ve.tensor_tensor(vec(T.Y, q), bq, T["wk%d" % bk][:, 0:TK], op=AluOpType.subtract).then_inc(T.sem["vw%d" % bk], 1)
                 vwc[bk] += 1
-                ready[c] = ("vw%d" % bk, vwc[bk])
+                done[q] = ("vw%d" % bk, vwc[bk])
+        if t > 0:
+            ybuf, ysm = vec(T.Y, t), done[t]
+    else:
+        if mine:
+            ve.memset(T.eye[:, :], 1.0).then_inc(T.sem.ms, 1)
+            wait("g", "ms", 1)
+            g.affine_select(T.eye[:, :], T.eye[:, :], [[-1, P]], AluOpType.is_equal, 0.0, 0, 1).then_inc(T.sem.idn, 1)
+            wait("t", "idn", 1)
 
-    def ysem(c):
-        wait("t", "y%d" % c, count(RELAY.get((c, J), c), group(J)))
+        for k, (c0, c1) in enumerate(mine):
+            bk = bank()
+            ps = T["wk%d" % bk]
+            for j, c in enumerate(range(c0, c1)):
+                wait("t", "l%d" % (c // 4), 16)
+                te.matmul(tile(ps, j), tile(T.L, c), T.eye[:, :], start=True, stop=True).then_inc(T.sem["pw%d" % bk], 1)
+                pwc[bk] += 1
+            wait("v", "pw%d" % bk, pwc[bk])
+            ve.tensor_copy(T.AT[:, P * (c0 - w):P * (c1 - w)], ps[:, 0:P * (c1 - c0)]).then_inc(T.sem["vw%d" % bk], 1)
+            vwc[bk] += 1
+            gsend.append(("vw%d" % bk, vwc[bk], T.AT[:, P * (c0 - w):P * (c1 - w)],
+                          T.AR[:, P * (MAXW * i + c0 - w):P * (MAXW * i + c1 - w)], later(t), "a%d_%d" % (i, k)))
 
-    pbuf, psem = T.bb, ("lb", 16)
-    if far:
-        for c in far:
-            ysem(c)
+        if i > 0:
+            for c0, c1 in [(c, c + 1) for c in range(t - 2, g0 - 1, -1)] + _split(w, g0):
+                cols = list(range(c0, c1))
+                bks = [bank() for c in cols]
+                ms = list(range(t - 1, max(c1, g0) - 1, -1))
+                for m in ms:
+                    for bk, c in zip(bks, cols):
+                        wait("t", "a%d_%d" % (m - g0, _chunk_of(m, c)), count(m, later(m)))
+                        rhs = xt("t", m)
+                        te.matmul(tile(T["wk%d" % bk], 0), tile(T.AR, MAXW * (m - g0) + c - w), rhs, start=(m == ms[0]),
+                                  stop=(m == ms[-1])).then_inc(T.sem["pw%d" % bk], 1)
+                        pwc[bk] += 1
+                for bk, c in zip(bks, cols):
+                    wait("v", "l%d" % (c // 4), 16)
+                    wait("v", "pw%d" % bk, pwc[bk])
+                    ve.tensor_tensor(tile(T.X, c), tile(T.L, c), tile(T["wk%d" % bk], 0),
+                                     op=AluOpType.subtract).then_inc(T.sem["vw%d" % bk], 1)
+                    vwc[bk] += 1
+                    ready[c] = ("vw%d" % bk, vwc[bk])
+
+        def ysem(c):
+            wait("t", "y%d" % c, count(RELAY.get((c, J), c), group(J)))
+
+        pbuf, psem = T.bb, ("lb", 16)
+        if far:
+            for c in far:
+                ysem(c)
+                lhs = xt("t", c)
+                te.matmul(T.accf[:, 0:TK], lhs, vec(T.Y, c), start=(c == far[0]), stop=(c == far[-1])).then_inc(T.sem.pf, 1)
+            wait("v", "pf", len(far))
+            wait("v", "lb", 16)
+            ve.tensor_tensor(T.pp[:, :], T.bb[:, :], T.accf[:, 0:TK], op=AluOpType.subtract).then_inc(T.sem.vp, 1)
+            pbuf, psem = T.pp, ("vp", 1)
+            if i < G - 1:
+                gsend.append(("vp", 1, T.pp[:, :], vec(T.PR, i), later(t)[::-1], "p%d" % i))
+
+        inq = [("p", q) for q in range(g0, t)]
+        win = [("y", c) for c in range(w, g0)]
+        near = (win + inq) if far else (inq + win)
+        for n, (kind, c) in enumerate(near):
+            if kind == "p":
+                wait("t", "p%d" % (c - g0), count(c, later(c)))
+                rhs = vec(T.PR, c - g0)
+            else:
+                ysem(c)
+                rhs = vec(T.Y, c)
             lhs = xt("t", c)
-            te.matmul(T.accf[:, 0:TK], lhs, vec(T.Y, c), start=(c == far[0]), stop=(c == far[-1])).then_inc(T.sem.pf, 1)
-        wait("v", "pf", len(far))
-        wait("v", "lb", 16)
-        ve.tensor_tensor(T.pp[:, :], T.bb[:, :], T.accf[:, 0:TK], op=AluOpType.subtract).then_inc(T.sem.vp, 1)
-        pbuf, psem = T.pp, ("vp", 1)
-        if i < G - 1:
-            gsend.append(("vp", 1, T.pp[:, :], vec(T.PR, i), later(t)[::-1], "p%d" % i))
-
-    inq = [("p", q) for q in range(g0, t)]
-    win = [("y", c) for c in range(w, g0)]
-    near = (win + inq) if far else (inq + win)
-    ybuf, ysm = pbuf[:, :], psem
-    for n, (kind, c) in enumerate(near):
-        if kind == "p":
-            wait("t", "p%d" % (c - g0), count(c, later(c)))
-            rhs = vec(T.PR, c - g0)
-        else:
-            ysem(c)
-            rhs = vec(T.Y, c)
-        lhs = xt("t", c)
-        te.matmul(T.acc[:, 0:TK], lhs, rhs, start=(n == 0), stop=(n == len(near) - 1)).then_inc(T.sem.pa, 1)
-    if near:
+            te.matmul(T.acc[:, 0:TK], lhs, rhs, start=(n == 0), stop=(n == len(near) - 1)).then_inc(T.sem.pa, 1)
         wait("v", "pa", len(near))
         wait("v", psem[0], psem[1])
         ve.tensor_tensor(vec(T.Y, t), pbuf[:, :], T.acc[:, 0:TK], op=AluOpType.subtract).then_inc(T.sem.vy, 1)
         ybuf, ysm = vec(T.Y, t), ("vy", 1)
 
-    wait("s", ysm[0], ysm[1])
-    sy.dma_start(T.y[:, :], ybuf).then_inc(T.sem.st, 16)
     for K in range(J + 1, len(GROUPS)):
         if (t, K) in RELAY:
             continue
@@ -265,6 +292,10 @@ def rank_program(g, core, T, topo):
     for sem, val, src, dst, dests, rsem in gsend:
         wait("g", sem, val)
         send(src, dst, dests, rsem)
+    wait("s", ysm[0], ysm[1])
+    if J < len(GROUPS) - 1 and sent[0]:
+        wait("s", "ls", sent[0])
+    sy.dma_start(T.y[:, :], ybuf).then_inc(T.sem.st, 16)
     if sent[0]:
         wait("g", "ls", sent[0])
     wait("s", "st", 16)

import numpy as np
from concourse.bass import DstId, RemoteDMATransfer
from concourse.mybir import AluOpType

N, TK, P = 16, 64, 128
GROUPS = [5, 3, 4, 4]
WINDOW = [0, 1, 1, 1]
NW = 6


def _plan():
    gs, s = [], 0
    for G in GROUPS:
        gs.append(s)
        s += G
    info = []
    for J, G in enumerate(GROUPS):
        for i in range(G):
            info.append((J, gs[J], G, i, gs[max(0, J - WINDOW[J])]))
    return gs, info


GS, INFO = _plan()


def _relays():
    r, nG = {}, len(GROUPS)
    if nG > 2 and GROUPS[0] > 1:
        r[(0, 2)] = GS[0] + GROUPS[0] - 1
    for J in range(1, nG - 1):
        c = J - 1
        if c < GROUPS[0] and nG - 1 > J and (c, nG - 1) not in r and (c, J) not in r:
            r[(c, nG - 1)] = GS[J] + GROUPS[J] - 1
    return r


RELAY = _relays()


def _split(a, b, n=4):
    return [(c0, min(c0 + n, b)) for c0 in range(a, b, n)]


def _chunks(m):
    J, g, G, i, w = INFO[m]
    if i == G - 1:
        return []
    return _split(g, m) + _split(w, g)


def _chunk_of(m, c):
    for k, (c0, c1) in enumerate(_chunks(m)):
        if c0 <= c < c1:
            return k
    return None


GMAX = max(GROUPS)
MAXW = max([1] + [m - INFO[m][4] for m in range(N) if _chunks(m)])
MAXK = max([1] + [len(_chunks(m)) for m in range(N)])

SCRATCH = {
    "L": ("sbuf", [P, P * (N - 1)], "float32"),
    "X": ("sbuf", [P, P * (N - 1)], "float32"),
    "AT": ("sbuf", [P, P * MAXW], "float32"),
    "AR": ("sbuf", [P, P * MAXW * max(1, GMAX - 1)], "float32"),
    "Y": ("sbuf", [P, TK * N], "float32"),
    "PR": ("sbuf", [P, TK * max(1, GMAX - 1)], "float32"),
    "bb": ("sbuf", [P, TK], "float32"),
    "pp": ("sbuf", [P, TK], "float32"),
    "eye": ("sbuf", [P, P], "float32"),
    "acc": ("psum", [P, 512], "float32"),
    "accf": ("psum", [P, 512], "float32"),
}
for _k in range(NW):
    SCRATCH["wk%d" % _k] = ("psum", [P, 512], "float32")

SEMAPHORES = (["lb", "ms", "idn", "ls", "st", "pa", "pf", "vp", "vy"]
              + ["l%d" % k for k in range(4)] + ["y%d" % s for s in range(N)]
              + ["p%d" % i for i in range(max(1, GMAX - 1))]
              + ["a%d_%d" % (i, k) for i in range(max(1, GMAX - 1)) for k in range(MAXK)]
              + ["pw%d" % k for k in range(NW)] + ["vw%d" % k for k in range(NW)])


def rank_program(g, core, T, topo):
    t = T.rank_of(core)
    if t is None:
        return
    cores = T.cores
    J, g0, G, i, w = INFO[t]
    te, ve, sy, sc = g.tensor, g.vector, g.sync, g.scalar
    qn = {"g": g, "t": te, "v": ve, "s": sy, "c": sc}
    seen = {}

    def wait(q, name, val):
        if seen.get((q, name), 0) < val:
            seen[(q, name)] = val
            qn[q].wait_ge(T.sem[name], val)

    def mask_of(src, dests):
        m = topo.mask(cores[src], cores[dests[0]])
        for d in dests[1:]:
            m &= topo.mask(cores[src], cores[d])
        return m

    def count(src, dests):
        return bin(mask_of(src, dests)).count("1")

    def later(m):
        return list(range(m + 1, INFO[m][1] + INFO[m][2]))

    def group(K):
        return list(range(GS[K], GS[K] + GROUPS[K]))

    sent = [0]

    def send(src_ap, dst_ap, dests, sem):
        ids = []
        for d in dests:
            rid, pid = topo.addr(cores[d], core)
            ids.append(DstId(rid=rid, pnc=pid))
        m = mask_of(t, dests)
        g.remote_dma_fused([RemoteDMATransfer(dst_ids=ids, dma_engine_mask=m, remote_sem=T.sem[sem], srcs=[src_ap],
                                              dsts=[dst_ap for _ in dests], alu_op=0)], local_sem=T.sem.ls)
        sent[0] += bin(m).count("1")

    def tile(buf, c):
        return buf[:, P * c:P * (c + 1)]

    def vec(buf, k):
        return buf[:, TK * k:TK * (k + 1)]

    mine = _chunks(t)
    sy.dma_start(T.bb[:, :], T.b[:, :]).then_inc(T.sem.lb, 16)
    for n, k in enumerate(list(range((t + 3) // 4))[::-1]):
        a, b = 512 * k, min(512 * (k + 1), P * t)
        (sc if n % 2 == 0 else sy).dma_start(T.L[:, a:b], T.l[:, a:b]).then_inc(T.sem["l%d" % k], 16)
    nb = [0]
    pwc, vwc = [0] * NW, [0] * NW

    def bank():
        k = nb[0] % NW
        nb[0] += 1
        wait("t", "vw%d" % k, vwc[k])
        return k

    ready = {}

    def modified(c):
        return i > 0 and w <= c <= t - 2

    def xt(q, c):
        if modified(c):
            wait(q, ready[c][0], ready[c][1])
            return tile(T.X, c)
        wait(q, "l%d" % (c // 4), 16)
        return tile(T.L, c)

    gsend = []
    far = list(range(0, w))
    if i < G - 1 and not far:
        gsend.append(("lb", 16, T.bb[:, :], vec(T.PR, i), later(t)[::-1], "p%d" % i))
    for (c, D), R in sorted(RELAY.items()):
        if R == t and INFO[c][0] == J:
            gsend.append(("p%d" % (c - g0), count(c, later(c)), vec(T.PR, c - g0), vec(T.Y, c), group(D), "y%d" % c))
        elif R == t:
            gsend.append(("y%d" % c, count(c, group(J)), vec(T.Y, c), vec(T.Y, c), group(D), "y%d" % c))

    ybuf, ysm = T.bb[:, :], ("lb", 16)

    if J == 0:
        for k, (c0, c1) in enumerate(mine):
            gsend.append(("l%d" % (c0 // 4), 16, T.L[:, P * c0:P * c1], T.AR[:, P * (MAXW * i + c0):P * (MAXW * i + c1)],
                          later(t)[::-1], "a%d_%d" % (i, k)))
        seq = [(t, 0)] if t >= 1 else []
        for q in range(1, t + 1):
            for c in range(q):
                if (q, c) not in seq:
                    seq.append((q, c))
        left = {q: q for q in range(1, t + 1)}
        rowbank, done = {}, {}
        for q, c in seq:
            first = q not in rowbank
            if first:
                rowbank[q] = bank()
            bk = rowbank[q]
            if q == t:
                wait("t", "l%d" % (c // 4), 16)
                lhs = tile(T.L, c)
            else:
                wait("t", "a%d_%d" % (q, _chunk_of(q, c)), count(q, later(q)))
                lhs = tile(T.AR, MAXW * q + c)
            if c == 0:
                wait("t", "p0", count(0, later(0)))
                rhs = vec(T.PR, 0)
            else:
                wait("t", done[c][0], done[c][1])
                rhs = vec(T.Y, c)
            left[q] -= 1
            te.matmul(T["wk%d" % bk][:, 0:TK], lhs, rhs, start=first, stop=(left[q] == 0)).then_inc(T.sem["pw%d" % bk], 1)
            pwc[bk] += 1
            if left[q] == 0:
                wait("v", "pw%d" % bk, pwc[bk])
                if q == t:
                    wait("v", "lb", 16)
                    bq = T.bb[:, :]
                else:
                    wait("v", "p%d" % q, count(q, later(q)))
                    bq = vec(T.PR, q)
                ve.tensor_tensor(vec(T.Y, q), bq, T["wk%d" % bk][:, 0:TK], op=AluOpType.subtract).then_inc(T.sem["vw%d" % bk], 1)
                vwc[bk] += 1
                done[q] = ("vw%d" % bk, vwc[bk])
        if t > 0:
            ybuf, ysm = vec(T.Y, t), done[t]
    else:
        if mine:
            ve.memset(T.eye[:, :], 1.0).then_inc(T.sem.ms, 1)
            wait("g", "ms", 1)
            g.affine_select(T.eye[:, :], T.eye[:, :], [[-1, P]], AluOpType.is_equal, 0.0, 0, 1).then_inc(T.sem.idn, 1)
            wait("t", "idn", 1)

        for k, (c0, c1) in enumerate(mine):
            bk = bank()
            ps = T["wk%d" % bk]
            for j, c in enumerate(range(c0, c1)):
                wait("t", "l%d" % (c // 4), 16)
                te.matmul(tile(ps, j), tile(T.L, c), T.eye[:, :], start=True, stop=True).then_inc(T.sem["pw%d" % bk], 1)
                pwc[bk] += 1
            wait("v", "pw%d" % bk, pwc[bk])
            ve.tensor_copy(T.AT[:, P * (c0 - w):P * (c1 - w)], ps[:, 0:P * (c1 - c0)]).then_inc(T.sem["vw%d" % bk], 1)
            vwc[bk] += 1
            gsend.append(("vw%d" % bk, vwc[bk], T.AT[:, P * (c0 - w):P * (c1 - w)],
                          T.AR[:, P * (MAXW * i + c0 - w):P * (MAXW * i + c1 - w)], later(t), "a%d_%d" % (i, k)))

        if i > 0:
            for c0, c1 in [(c, c + 1) for c in range(t - 2, g0 - 1, -1)] + _split(w, g0):
                cols = list(range(c0, c1))
                bks = [bank() for c in cols]
                ms = list(range(t - 1, max(c1, g0) - 1, -1))
                for m in ms:
                    for bk, c in zip(bks, cols):
                        wait("t", "a%d_%d" % (m - g0, _chunk_of(m, c)), count(m, later(m)))
                        rhs = xt("t", m)
                        te.matmul(tile(T["wk%d" % bk], 0), tile(T.AR, MAXW * (m - g0) + c - w), rhs, start=(m == ms[0]),
                                  stop=(m == ms[-1])).then_inc(T.sem["pw%d" % bk], 1)
                        pwc[bk] += 1
                for bk, c in zip(bks, cols):
                    wait("v", "l%d" % (c // 4), 16)
                    wait("v", "pw%d" % bk, pwc[bk])
                    ve.tensor_tensor(tile(T.X, c), tile(T.L, c), tile(T["wk%d" % bk], 0),
                                     op=AluOpType.subtract).then_inc(T.sem["vw%d" % bk], 1)
                    vwc[bk] += 1
                    ready[c] = ("vw%d" % bk, vwc[bk])

        def ysem(c):
            wait("t", "y%d" % c, count(RELAY.get((c, J), c), group(J)))

        pbuf, psem = T.bb, ("lb", 16)
        if far:
            for c in far:
                ysem(c)
                lhs = xt("t", c)
                te.matmul(T.accf[:, 0:TK], lhs, vec(T.Y, c), start=(c == far[0]), stop=(c == far[-1])).then_inc(T.sem.pf, 1)
            wait("v", "pf", len(far))
            wait("v", "lb", 16)
            ve.tensor_tensor(T.pp[:, :], T.bb[:, :], T.accf[:, 0:TK], op=AluOpType.subtract).then_inc(T.sem.vp, 1)
            pbuf, psem = T.pp, ("vp", 1)
            if i < G - 1:
                gsend.append(("vp", 1, T.pp[:, :], vec(T.PR, i), later(t)[::-1], "p%d" % i))

        inq = [("p", q) for q in range(g0, t)]
        win = [("y", c) for c in range(w, g0)]
        near = (win + inq) if far else (inq + win)
        for n, (kind, c) in enumerate(near):
            if kind == "p":
                wait("t", "p%d" % (c - g0), count(c, later(c)))
                rhs = vec(T.PR, c - g0)
            else:
                ysem(c)
                rhs = vec(T.Y, c)
            lhs = xt("t", c)
            te.matmul(T.acc[:, 0:TK], lhs, rhs, start=(n == 0), stop=(n == len(near) - 1)).then_inc(T.sem.pa, 1)
        wait("v", "pa", len(near))
        wait("v", psem[0], psem[1])
        ve.tensor_tensor(vec(T.Y, t), pbuf[:, :], T.acc[:, 0:TK], op=AluOpType.subtract).then_inc(T.sem.vy, 1)
        ybuf, ysm = vec(T.Y, t), ("vy", 1)

    for K in range(J + 1, len(GROUPS)):
        if (t, K) in RELAY:
            continue
        gsend.append((ysm[0], ysm[1], ybuf, vec(T.Y, t), group(K)[::-1] if K == J + 1 else group(K), "y%d" % t))
    for sem, val, src, dst, dests, rsem in gsend:
        wait("g", sem, val)
        send(src, dst, dests, rsem)
    wait("s", ysm[0], ysm[1])
    if J < len(GROUPS) - 1 and sent[0]:
        wait("s", "ls", sent[0])
    sy.dma_start(T.y[:, :], ybuf).then_inc(T.sem.st, 16)
    if sent[0]:
        wait("g", "ls", sent[0])
    wait("s", "st", 16)
